import numpy as np, ml_dtypes
CORES = [129,145,193,257,273,321,385,401,449]
N = 9
DEG, TK = 5, 128
MASK = [[0,2,6,7,8],[0,1,5,7,8],[0,1,2,6,8],[0,1,3,6,8],[1,2,3,4,8],[1,4,5,6,7],[1,2,5,6,8],[1,3,5,6,7],[1,2,5,7,8]]
def setup_inputs(rng):
    return {"x": rng.standard_normal((N, 128, TK), dtype=np.float32).astype(ml_dtypes.bfloat16), "w": rng.standard_normal((N, 128, DEG * 128), dtype=np.float32).astype(ml_dtypes.bfloat16)}
def setup_inputs_big(rng):
    d = setup_inputs(rng)
    for k in ("x", "w"): d[k] = (d[k].astype(np.float32) * 1024.0).astype(d[k].dtype)
    return d
def setup_inputs_small(rng):
    d = setup_inputs(rng)
    for k in ("x", "w"): d[k] = (d[k].astype(np.float32) * (1 / 1024.0)).astype(d[k].dtype)
    return d
def setup_inputs_apart(rng):
    d = setup_inputs(rng)
    f = (10.0 ** rng.permutation(np.linspace(-1.5, 1.5, N))).astype(np.float32).reshape(N, 1, 1)
    for k in ("x", "w"): d[k] = (d[k].astype(np.float32) * f).astype(d[k].dtype)
    return d
def reference(x, w):
    X, W = x.astype(np.float64), w.astype(np.float64)
    y = np.zeros((N, 128, TK))
    for r in range(N):
        for i, j in enumerate(MASK[r]):
            y[r] += W[r][:, 128 * i:128 * i + 128].T @ X[j]
    return {"y": y.astype(ml_dtypes.bfloat16 if x.dtype != np.float64 else np.float64)}

@@ -1,0 +1,143 @@
+from concourse.bass import DstId, RemoteDMATransfer
+
+N, DEG, TK = 9, 5, 128
+
+SCRATCH = {
+    "xs": ("sbuf", [128, N * TK], "bfloat16"),
+    "ws": ("sbuf", [128, DEG * 128], "bfloat16"),
+    "ys": ("sbuf", [128, TK], "bfloat16"),
+    "acc": ("psum", [128, TK], "float32"),
+}
+SEMAPHORES = ["xl", "wl", "mm", "cp", "st", "snt"] + ["a%d" % j for j in range(N)]
+
+_CACHE = {}
+
+
+def _bits(m):
+    return [b for b in range(m.bit_length()) if (m >> b) & 1]
+
+
+def _mask_of(bits):
+    m = 0
+    for b in bits:
+        m |= 1 << b
+    return m
+
+
+def _plan(T, topo):
+    cores, need = T.cores, T.tables["MASK"]
+    n = len(cores)
+
+    def ok(a, b):
+        return a != b and topo.may_write(cores[a], cores[b])
+
+    direct = [[r for r in range(n) if j in need[r] and ok(j, r)] for j in range(n)]
+    missing = [set(j for j in need[r] if j != r and not ok(j, r)) for r in range(n)]
+    have = [set(j for j in need[m] if j == m or ok(j, m)) for m in range(n)]
+    forwards, load, passes = [[] for _ in range(n)], [0] * n, [set() for _ in range(n)]
+    while any(missing):
+        groups = {}
+        for m in range(n):
+            for r in range(n):
+                tiles = tuple(sorted(missing[r] & have[m])) if ok(m, r) else ()
+                if tiles:
+                    groups.setdefault((m, tiles), []).append(r)
+        if not groups:
+            raise ValueError("a tile cannot reach its destination in two hops")
+        m, tiles = min(groups, key=lambda k: (-len(k[1]) * len(groups[k]), load[k[0]], len(set(k[1]) - passes[k[0]]), k))
+        dsts = groups[(m, tiles)]
+        forwards[m].append((tiles, dsts))
+        load[m] += len(dsts)
+        passes[m] |= set(tiles)
+        for r in dsts:
+            missing[r] -= set(tiles)
+    order = []
+    for m in range(n):
+        for tiles, _ in forwards[m]:
+            if len(tiles) > 1:
+                if any(j in order for j in tiles):
+                    raise ValueError("two bundles share a tile: no slot order")
+                order += list(tiles)
+    order += [j for j in range(n) if j not in order]
+    slot = [order.index(j) for j in range(n)]
+
+    def engines(j, dsts):
+        m = topo.mask(cores[j], cores[dsts[0]])
+        for r in dsts:
+            m &= topo.mask(cores[j], cores[r])
+        return _bits(m)
+
+    sends, stages = [[] for _ in range(n)], [[] for _ in range(n)]
+    for j in range(n):
+        first = [r for r in direct[j] if j in passes[r]]
+        rest = [r for r in direct[j] if j not in passes[r]]
+        eng = engines(j, direct[j])
+        if first and rest:
+            parts = [(first, eng[0::2], 1), (rest, eng[1::2], 2)]
+        else:
+            parts = [(first + rest, eng, 1 if first else 2)]
+        for dsts, e, stage in parts:
+            sends[j].append(((j,), dsts, _mask_of(e), ()))
+            for r in dsts:
+                stages[r].append((stage, (j,), len(e)))
+    for m in range(n):
+        for k, (tiles, dsts) in enumerate(sorted(forwards[m], key=lambda f: -len(f[0]))):
+            e = engines(m, dsts)
+            sends[m].append((tiles, dsts, _mask_of(e), tuple(j for j in tiles if j != m)))
+            for r in dsts:
+                stages[r].append((3 + k, tiles, len(e)))
+    arrive = [[(tiles, inc) for _, tiles, inc in sorted(stages[r])] for r in range(n)]
+    return sends, arrive, slot
+
+
+def rank_program(g, core, T, topo):
+    rank = T.rank_of(core)
+    if rank is None:
+        return
+    if "plan" not in _CACHE:
+        _CACHE["plan"] = _plan(T, topo)
+    sends, arrive, slot = _CACHE["plan"]
+    need = T.tables["MASK"][rank]
+    sem = T.sem
+
+    def tile(j, k=1):
+        return T.xs[:, slot[j] * TK:(slot[j] + k) * TK]
+
+    g.sync.dma_start(tile(rank), T.x[:, :]).then_inc(sem.xl, 16)
+    g.sync.dma_start(T.ws[:, :], T.w[:, :]).then_inc(sem.wl, 16)
+
+    incs = dict((tiles[0], inc) for tiles, inc in arrive[rank])
+    g.wait_ge(sem.xl, 16)
+    left = 0
+    for tiles, dsts, mask, waits in sends[rank]:
+        for j in waits:
+            g.wait_ge(sem["a%d" % j], incs[j])
+        ids = []
+        for r in dsts:
+            rid, pid = topo.addr(T.cores[r], core)
+            ids.append(DstId(rid=rid, pnc=pid))
+        ap = tile(tiles[0], len(tiles))
+        g.remote_dma_fused([RemoteDMATransfer(dst_ids=ids, dma_engine_mask=mask, remote_sem=sem["a%d" % tiles[0]],
+                                              srcs=[ap], dsts=[ap for _ in dsts], alu_op=0)], local_sem=sem.snt)
+        left += len(_bits(mask))
+
+    todo = [((rank,), 0)] + arrive[rank]
+    done, total = 0, sum(len(tiles) for tiles, _ in todo)
+    g.tensor.wait_ge(sem.xl, 16)
+    g.tensor.wait_ge(sem.wl, 16)
+    for tiles, inc in todo:
+        if inc:
+            g.tensor.wait_ge(sem["a%d" % tiles[0]], inc)
+        for j in tiles:
+            i = need.index(j)
+            done += 1
+            mm = g.tensor.matmul(T.acc[:, :], T.ws[:, i * 128:(i + 1) * 128], tile(j), done == 1, done == total)
+    mm.then_inc(sem.mm, 1)
+
+    g.vector.wait_ge(sem.mm, 1)
+    g.vector.tensor_copy(T.ys[:, :], T.acc[:, :]).then_inc(sem.cp, 1)
+    g.sync.wait_ge(sem.cp, 1)
+    g.sync.dma_start(T.y[:, :], T.ys[:, :]).then_inc(sem.st, 16)
+    g.sync.wait_ge(sem.st, 16)
+    if left:
+        g.wait_ge(sem.snt, left)

@@ -13,15 +13,19 @@ SEMAPHORES = ["xl", "wl", "mm", "cp", "st", "snt"] + ["a%d" % j for j in range(N
 _CACHE = {}
 
 
-def _bits(m):
-    return [b for b in range(m.bit_length()) if (m >> b) & 1]
+def _count(m):
+    return sum((m >> b) & 1 for b in range(m.bit_length()))
 
 
-def _mask_of(bits):
-    m = 0
-    for b in bits:
-        m |= 1 << b
-    return m
+def _world(topo):
+    h = 0
+    while True:
+        try:
+            topo.rack(h)
+        except ValueError:
+            break
+        h += 1
+    return range(h * topo.CORES_PER_HOST)
 
 
 def _plan(T, topo):
@@ -29,115 +33,117 @@ def _plan(T, topo):
     n = len(cores)
 
     def ok(a, b):
-        return a != b and topo.may_write(cores[a], cores[b])
+        return a != b and topo.may_write(a, b)
 
-    direct = [[r for r in range(n) if j in need[r] and ok(j, r)] for j in range(n)]
-    missing = [set(j for j in need[r] if j != r and not ok(j, r)) for r in range(n)]
-    have = [set(j for j in need[m] if j == m or ok(j, m)) for m in range(n)]
-    forwards, load, passes = [[] for _ in range(n)], [0] * n, [set() for _ in range(n)]
-    while any(missing):
-        groups = {}
-        for m in range(n):
-            for r in range(n):
-                tiles = tuple(sorted(missing[r] & have[m])) if ok(m, r) else ()
-                if tiles:
-                    groups.setdefault((m, tiles), []).append(r)
-        if not groups:
-            raise ValueError("a tile cannot reach its destination in two hops")
-        m, tiles = min(groups, key=lambda k: (-len(k[1]) * len(groups[k]), load[k[0]], len(set(k[1]) - passes[k[0]]), k))
-        dsts = groups[(m, tiles)]
-        forwards[m].append((tiles, dsts))
-        load[m] += len(dsts)
-        passes[m] |= set(tiles)
-        for r in dsts:
-            missing[r] -= set(tiles)
-    order = []
-    for m in range(n):
-        for tiles, _ in forwards[m]:
-            if len(tiles) > 1:
-                if any(j in order for j in tiles):
-                    raise ValueError("two bundles share a tile: no slot order")
-                order += list(tiles)
-    order += [j for j in range(n) if j not in order]
-    slot = [order.index(j) for j in range(n)]
+    direct = [[r for r in range(n) if j in need[r] and ok(cores[j], cores[r])] for j in range(n)]
+    miss = [[r for r in range(n) if j in need[r] and r != j and not ok(cores[j], cores[r])] for j in range(n)]
+    own = [len(d) for d in direct]
+    cap = max(own)
+    early = 2
+    nfw = [0] * n
+    passes = dict((c, []) for c in cores)
+    helper = {}
+    taken = set(cores)
+    busy_hosts = set(topo.host(c) for c in cores)
+    for j in sorted((j for j in range(n) if miss[j]), key=lambda j: (-own[j], j)):
+        left, by = list(miss[j]), {}
+        while True:
+            pairs = [(topo.chip(cores[m]) != topo.chip(cores[r]), nfw[m], r, m) for r in left for m in direct[j]
+                     if ok(cores[m], cores[r]) and max(own[m], early) + nfw[m] + 1 <= cap]
+            if not pairs:
+                break
+            _, _, r, m = min(pairs)
+            by.setdefault(m, []).append(r)
+            nfw[m] += 1
+            left.remove(r)
+        for m in by:
+            passes[cores[m]].append((j, by[m]))
+        if left:
+            o = cores[j]
+            c = min(c for c in _world(topo) if c not in taken and topo.host(c) not in busy_hosts and ok(o, c)
+                    and topo.chip(c) == topo.chip(o) and topo.die(c) == topo.die(o)
+                    and all(ok(c, cores[r]) for r in left))
+            taken.add(c)
+            helper[j] = c
+            passes[c] = [(j, left)]
 
-    def engines(j, dsts):
-        m = topo.mask(cores[j], cores[dsts[0]])
-        for r in dsts:
-            m &= topo.mask(cores[j], cores[r])
-        return _bits(m)
+    def mask(src, dsts):
+        m = topo.mask(src, dsts[0])
+        for d in dsts:
+            m &= topo.mask(src, d)
+        return m
 
-    sends, stages = [[] for _ in range(n)], [[] for _ in range(n)]
+    sends, when, inc = dict((c, []) for c in passes), {}, {}
+    free = dict((c, 0) for c in passes)
+
+    def call(src, j, dsts, wait):
+        m = mask(src, dsts)
+        sends[src].append((j, dsts, m, wait))
+        free[src] += len(dsts)
+        for d in dsts:
+            when[(j, d)] = free[src]
+            inc[(j, d)] = _count(m)
+
     for j in range(n):
-        first = [r for r in direct[j] if j in passes[r]]
-        rest = [r for r in direct[j] if j not in passes[r]]
-        eng = engines(j, direct[j])
-        if first and rest:
-            parts = [(first, eng[0::2], 1), (rest, eng[1::2], 2)]
-        else:
-            parts = [(first + rest, eng, 1 if first else 2)]
-        for dsts, e, stage in parts:
-            sends[j].append(((j,), dsts, _mask_of(e), ()))
-            for r in dsts:
-                stages[r].append((stage, (j,), len(e)))
-    for m in range(n):
-        for k, (tiles, dsts) in enumerate(sorted(forwards[m], key=lambda f: -len(f[0]))):
-            e = engines(m, dsts)
-            sends[m].append((tiles, dsts, _mask_of(e), tuple(j for j in tiles if j != m)))
-            for r in dsts:
-                stages[r].append((3 + k, tiles, len(e)))
-    arrive = [[(tiles, inc) for _, tiles, inc in sorted(stages[r])] for r in range(n)]
-    return sends, arrive, slot
+        relays = [cores[r] for r in direct[j] if any(t == j for t, _ in passes[cores[r]])]
+        rest = [cores[r] for r in direct[j] if cores[r] not in relays]
+        for dsts in ([helper[j]] if j in helper else [], relays, rest):
+            if dsts:
+                call(cores[j], j, dsts, False)
+    for c in passes:
+        for j, dsts in sorted(passes[c], key=lambda p: when[(p[0], c)]):
+            free[c] = max(free[c], when[(j, c)] + (1 if c in cores else 2))
+            call(c, j, [cores[r] for r in dsts], True)
+    arrive = [sorted((j for j in need[r] if j != r), key=lambda j: (when[(j, cores[r])], j)) for r in range(n)]
+    return sends, arrive, inc
 
 
 def rank_program(g, core, T, topo):
-    rank = T.rank_of(core)
-    if rank is None:
-        return
     if "plan" not in _CACHE:
         _CACHE["plan"] = _plan(T, topo)
-    sends, arrive, slot = _CACHE["plan"]
-    need = T.tables["MASK"][rank]
+    sends, arrive, inc = _CACHE["plan"]
+    if core not in sends:
+        return
+    rank = T.rank_of(core)
     sem = T.sem
 
-    def tile(j, k=1):
-        return T.xs[:, slot[j] * TK:(slot[j] + k) * TK]
+    def tile(j):
+        return T.xs[:, j * TK:(j + 1) * TK]
 
-    g.sync.dma_start(tile(rank), T.x[:, :]).then_inc(sem.xl, 16)
-    g.sync.dma_start(T.ws[:, :], T.w[:, :]).then_inc(sem.wl, 16)
+    if rank is not None:
+        g.sync.dma_start(tile(rank), T.x[:, :]).then_inc(sem.xl, 16)
+        g.sync.dma_start(T.ws[:, :], T.w[:, :]).then_inc(sem.wl, 16)
+        g.wait_ge(sem.xl, 16)
 
-    incs = dict((tiles[0], inc) for tiles, inc in arrive[rank])
-    g.wait_ge(sem.xl, 16)
     left = 0
-    for tiles, dsts, mask, waits in sends[rank]:
-        for j in waits:
-            g.wait_ge(sem["a%d" % j], incs[j])
+    for j, dsts, mask, wait in sends[core]:
+        if wait:
+            g.wait_ge(sem["a%d" % j], inc[(j, core)])
         ids = []
-        for r in dsts:
-            rid, pid = topo.addr(T.cores[r], core)
+        for d in dsts:
+            rid, pid = topo.addr(d, core)
             ids.append(DstId(rid=rid, pnc=pid))
-        ap = tile(tiles[0], len(tiles))
-        g.remote_dma_fused([RemoteDMATransfer(dst_ids=ids, dma_engine_mask=mask, remote_sem=sem["a%d" % tiles[0]],
-                                              srcs=[ap], dsts=[ap for _ in dsts], alu_op=0)], local_sem=sem.snt)
-        left += len(_bits(mask))
+        g.remote_dma_fused([RemoteDMATransfer(dst_ids=ids, dma_engine_mask=mask, remote_sem=sem["a%d" % j],
+                                              srcs=[tile(j)], dsts=[tile(j) for _ in dsts], alu_op=0)],
+                           local_sem=sem.snt)
+        left += _count(mask)
 
-    todo = [((rank,), 0)] + arrive[rank]
-    done, total = 0, sum(len(tiles) for tiles, _ in todo)
-    g.tensor.wait_ge(sem.xl, 16)
-    g.tensor.wait_ge(sem.wl, 16)
-    for tiles, inc in todo:
-        if inc:
-            g.tensor.wait_ge(sem["a%d" % tiles[0]], inc)
-        for j in tiles:
+    if rank is not None:
+        need = T.tables["MASK"][rank]
+        todo = [rank] + arrive[rank]
+        g.tensor.wait_ge(sem.xl, 16)
+        g.tensor.wait_ge(sem.wl, 16)
+        for k, j in enumerate(todo):
+            if j != rank:
+                g.tensor.wait_ge(sem["a%d" % j], inc[(j, core)])
             i = need.index(j)
-            done += 1
-            mm = g.tensor.matmul(T.acc[:, :], T.ws[:, i * 128:(i + 1) * 128], tile(j), done == 1, done == total)
-    mm.then_inc(sem.mm, 1)
+            mm = g.tensor.matmul(T.acc[:, :], T.ws[:, i * 128:(i + 1) * 128], tile(j), k == 0, k == len(todo) - 1)
+        mm.then_inc(sem.mm, 1)
 
-    g.vector.wait_ge(sem.mm, 1)
-    g.vector.tensor_copy(T.ys[:, :], T.acc[:, :]).then_inc(sem.cp, 1)
-    g.sync.wait_ge(sem.cp, 1)
-    g.sync.dma_start(T.y[:, :], T.ys[:, :]).then_inc(sem.st, 16)
-    g.sync.wait_ge(sem.st, 16)
+        g.vector.wait_ge(sem.mm, 1)
+        g.vector.tensor_copy(T.ys[:, :], T.acc[:, :]).then_inc(sem.cp, 1)
+        g.sync.wait_ge(sem.cp, 1)
+        g.sync.dma_start(T.y[:, :], T.ys[:, :]).then_inc(sem.st, 16)
+        g.sync.wait_ge(sem.st, 16)
     if left:
         g.wait_ge(sem.snt, left)

from concourse.bass import DstId, RemoteDMATransfer

N, DEG, TK = 9, 5, 128

SCRATCH = {
    "xs": ("sbuf", [128, N * TK], "bfloat16"),
    "ws": ("sbuf", [128, DEG * 128], "bfloat16"),
    "ys": ("sbuf", [128, TK], "bfloat16"),
    "acc": ("psum", [128, TK], "float32"),
}
SEMAPHORES = ["xl", "wl", "mm", "cp", "st", "snt"] + ["a%d" % j for j in range(N)]

_CACHE = {}


def _count(m):
    return sum((m >> b) & 1 for b in range(m.bit_length()))


def _world(topo):
    h = 0
    while True:
        try:
            topo.rack(h)
        except ValueError:
            break
        h += 1
    return range(h * topo.CORES_PER_HOST)


def _plan(T, topo):
    cores, need = T.cores, T.tables["MASK"]
    n = len(cores)

    def ok(a, b):
        return a != b and topo.may_write(a, b)

    direct = [[r for r in range(n) if j in need[r] and ok(cores[j], cores[r])] for j in range(n)]
    miss = [[r for r in range(n) if j in need[r] and r != j and not ok(cores[j], cores[r])] for j in range(n)]
    own = [len(d) for d in direct]
    cap = max(own)
    early = 2
    nfw = [0] * n
    passes = dict((c, []) for c in cores)
    helper = {}
    taken = set(cores)
    busy_hosts = set(topo.host(c) for c in cores)
    for j in sorted((j for j in range(n) if miss[j]), key=lambda j: (-own[j], j)):
        left, by = list(miss[j]), {}
        while True:
            pairs = [(topo.chip(cores[m]) != topo.chip(cores[r]), nfw[m], r, m) for r in left for m in direct[j]
                     if ok(cores[m], cores[r]) and max(own[m], early) + nfw[m] + 1 <= cap]
            if not pairs:
                break
            _, _, r, m = min(pairs)
            by.setdefault(m, []).append(r)
            nfw[m] += 1
            left.remove(r)
        for m in by:
            passes[cores[m]].append((j, by[m]))
        if left:
            o = cores[j]
            c = min(c for c in _world(topo) if c not in taken and topo.host(c) not in busy_hosts and ok(o, c)
                    and topo.chip(c) == topo.chip(o) and topo.die(c) == topo.die(o)
                    and all(ok(c, cores[r]) for r in left))
            taken.add(c)
            helper[j] = c
            passes[c] = [(j, left)]

    def mask(src, dsts):
        m = topo.mask(src, dsts[0])
        for d in dsts:
            m &= topo.mask(src, d)
        return m

    sends, when, inc = dict((c, []) for c in passes), {}, {}
    free = dict((c, 0) for c in passes)

    def call(src, j, dsts, wait):
        m = mask(src, dsts)
        sends[src].append((j, dsts, m, wait))
        free[src] += len(dsts)
        for d in dsts:
            when[(j, d)] = free[src]
            inc[(j, d)] = _count(m)

    for j in range(n):
        relays = [cores[r] for r in direct[j] if any(t == j for t, _ in passes[cores[r]])]
        rest = [cores[r] for r in direct[j] if cores[r] not in relays]
        for dsts in ([helper[j]] if j in helper else [], relays, rest):
            if dsts:
                call(cores[j], j, dsts, False)
    for c in passes:
        for j, dsts in sorted(passes[c], key=lambda p: when[(p[0], c)]):
            free[c] = max(free[c], when[(j, c)] + (1 if c in cores else 2))
            call(c, j, [cores[r] for r in dsts], True)
    arrive = [sorted((j for j in need[r] if j != r), key=lambda j: (when[(j, cores[r])], j)) for r in range(n)]
    return sends, arrive, inc


def rank_program(g, core, T, topo):
    if "plan" not in _CACHE:
        _CACHE["plan"] = _plan(T, topo)
    sends, arrive, inc = _CACHE["plan"]
    if core not in sends:
        return
    rank = T.rank_of(core)
    sem = T.sem

    def tile(j):
        return T.xs[:, j * TK:(j + 1) * TK]

    if rank is not None:
        g.sync.dma_start(tile(rank), T.x[:, :]).then_inc(sem.xl, 16)
        g.sync.dma_start(T.ws[:, :], T.w[:, :]).then_inc(sem.wl, 16)
        g.wait_ge(sem.xl, 16)

    left = 0
    for j, dsts, mask, wait in sends[core]:
        if wait:
            g.wait_ge(sem["a%d" % j], inc[(j, core)])
        ids = []
        for d in dsts:
            rid, pid = topo.addr(d, core)
            ids.append(DstId(rid=rid, pnc=pid))
        g.remote_dma_fused([RemoteDMATransfer(dst_ids=ids, dma_engine_mask=mask, remote_sem=sem["a%d" % j],
                                              srcs=[tile(j)], dsts=[tile(j) for _ in dsts], alu_op=0)],
                           local_sem=sem.snt)
        left += _count(mask)

    if rank is not None:
        need = T.tables["MASK"][rank]
        todo = [rank] + arrive[rank]
        g.tensor.wait_ge(sem.xl, 16)
        g.tensor.wait_ge(sem.wl, 16)
        for k, j in enumerate(todo):
            if j != rank:
                g.tensor.wait_ge(sem["a%d" % j], inc[(j, core)])
            i = need.index(j)
            mm = g.tensor.matmul(T.acc[:, :], T.ws[:, i * 128:(i + 1) * 128], tile(j), k == 0, k == len(todo) - 1)
        mm.then_inc(sem.mm, 1)

        g.vector.wait_ge(sem.mm, 1)
        g.vector.tensor_copy(T.ys[:, :], T.acc[:, :]).then_inc(sem.cp, 1)
        g.sync.wait_ge(sem.cp, 1)
        g.sync.dma_start(T.y[:, :], T.ys[:, :]).then_inc(sem.st, 16)
        g.sync.wait_ge(sem.st, 16)
    if left:
        g.wait_ge(sem.snt, left)
